import numpy as np
import ml_dtypes


def mxq(x, axis, fmt="e4m3"):
    dtype, down = {"e4m3": (ml_dtypes.float8_e4m3fn, 7), "e5m2": (ml_dtypes.float8_e5m2, 14)}[fmt]
    v = np.moveaxis(np.asarray(x, np.float32).astype(ml_dtypes.bfloat16).astype(np.float64), axis, -1)
    blocks = v.reshape(v.shape[:-1] + (-1, 32))
    amax = np.abs(blocks).max(-1, keepdims=True)
    byte = np.maximum(np.where(amax > 0, np.frexp(amax)[1] - 1 + 127, 0) - down, 1)
    scale = np.exp2(byte - 127.0)
    codes = (blocks / scale).astype(np.float32).astype(dtype).astype(np.float64)
    return np.moveaxis((codes * scale).reshape(v.shape), -1, axis)


WIDE = False


def mx_kscale(k):
    if not WIDE:
        return np.ones(k)
    levels = np.array([30, -30])
    if k % 512:
        return np.exp2(np.random.permutation(np.resize(levels, k // 32))).repeat(32)
    a = np.empty((k // 512, 16))
    for p in range(k // 512):
        a[p, :8] = np.random.permutation(np.resize(levels, 8))
        for g in range(8):
            far = levels[np.abs(levels - a[p, g]) >= 10]
            a[p, g + 8] = far[np.random.randint(len(far))]
    return np.exp2(a.ravel()).repeat(32)


def f64(x):
    return np.asarray(x).astype(np.float64)


def striped(idx):
    return np.tile(np.asarray(idx).reshape(-1, 16).T, (8, 1)).astype(np.uint16)


def unstriped(offs):
    return offs[:16].T.reshape(-1).astype(np.int64)


def striped8(idx):
    return np.asarray(idx).reshape(8, -1, 16).transpose(0, 2, 1).reshape(128, -1).astype(np.uint16)


def unstriped8(offs):
    return offs.reshape(8, 16, -1).transpose(0, 2, 1).reshape(8, -1).astype(np.int64)


def pick8(x, idx, run):
    r = np.arange(len(x))
    return x[r[:, None], idx[r % (8 * run) // run]]


E2M1 = np.array([0.0, 0.5, 1.0, 1.5, 2.0, 3.0, 4.0, 6.0, -0.0, -0.5, -1.0, -1.5, -2.0, -3.0, -4.0, -6.0])


def pack_weight(w, fmt):
    k, n = w.shape
    w = f64(np.asarray(w, np.float32).astype(ml_dtypes.bfloat16)).reshape(k // 32, 32, n)
    amax = np.abs(w).max(1)
    if fmt in ("e4m3", "e5m2"):
        byte = np.frexp(amax)[1] - 1 + 127 - (7 if fmt == "e4m3" else 14)
    else:
        mant, ex = np.frexp(amax / 6.0)
        byte = np.where(mant > 0.5, ex, ex - 1) + 127
    byte = np.clip(np.where(amax > 0, byte, 1), 1, 254)
    scaled = (w * np.exp2(127.0 - byte)[:, None, :]).reshape(k, n).astype(np.float32)
    by_word = np.ascontiguousarray(scaled.reshape(k // 512, 128, 4, n).transpose(0, 1, 3, 2))
    if fmt in ("e4m3", "e5m2"):
        words = by_word.astype(ml_dtypes.float8_e4m3fn if fmt == "e4m3" else ml_dtypes.float8_e5m2).view(np.uint8)
    else:
        c = by_word.astype(ml_dtypes.float4_e2m1fn).view(np.uint8) & 0xF
        words = (c[..., 0::2] | (c[..., 1::2] << 4)).reshape(k // 512, 128, 2 * n)
    return np.ascontiguousarray(words), np.ascontiguousarray(byte.astype(np.uint8).reshape(k // 512, 16, n))


def unpack_weight(words, scales, fmt):
    g, _, n = scales.shape
    words = np.ascontiguousarray(words).reshape(g, 128, n, -1)
    if fmt in ("e4m3", "e5m2"):
        vals = words.view(ml_dtypes.float8_e4m3fn if fmt == "e4m3" else ml_dtypes.float8_e5m2).astype(np.float64)
    else:
        nib = np.empty((g, 128, n, 4), np.uint8)
        nib[..., 0::2] = words & 0xF
        nib[..., 1::2] = words >> 4
        vals = E2M1[nib]
    vals = vals * np.repeat(np.exp2(scales.astype(np.float64) - 127.0), 8, axis=1)[..., None]
    return vals.transpose(0, 1, 3, 2).reshape(g * 512, n)


def sgn(shape):
    return np.random.uniform(0.5, 2.0, shape) * np.where(np.random.standard_normal(shape) < 0, -1.0, 1.0)


K, T, J, R, V, C, O, N, E = 512, 1024, 256, 512, 1024, 512, 256, 256, 1024


def setup_inputs():
    n = np.random.standard_normal
    idx = np.random.permutation(V)[:R]
    idx2 = np.random.permutation(T)[:J]
    idx3 = np.stack([np.random.permutation(C)[:J] for _ in range(8)])
    idx4 = np.random.permutation(C)[:C]
    idx5 = np.random.permutation(C)[:O]
    idx6 = np.random.permutation(T)[:O]
    idx7 = np.random.permutation(E)[:O]
    fk = mx_kscale(K)
    fr = mx_kscale(R)
    tr = np.ones(V)
    tr[idx] = fr
    xtp = pack_weight(n((K, T)) / fk[:, None], "e4m3")
    wtp = pack_weight(n((K, V)) * 1 / np.sqrt(K) * fk[:, None] * tr, "e2m1")
    wbp = pack_weight(n((R, N)) * 1 / np.sqrt(R) / fr[:, None], "e5m2")
    wsp = pack_weight(n((K, N)) * 1 / np.sqrt(K) * fk[:, None], "e5m2")
    return {
        "xt_words": xtp[0],
        "xt_scales": xtp[1],
        "wt_words": wtp[0],
        "wt_scales": wtp[1],
        "sa": (sgn((R, 1))).astype(np.float32),
        "wb_words": wbp[0],
        "wb_scales": wbp[1],
        "ws_words": wsp[0],
        "ws_scales": wsp[1],
        "offs": striped(idx),
        "offs2": striped(idx2),
        "offs3": striped8(idx3),
        "offs4": striped(idx4),
        "offs5": striped(idx5),
        "offs6": striped(idx6),
        "offs7": striped(idx7),
    }


def reference(xt_words, xt_scales, wt_words, wt_scales, sa, wb_words, wb_scales, ws_words, ws_scales, offs, offs2, offs3, offs4, offs5, offs6, offs7):
    idx = unstriped(offs)
    idx2 = unstriped(offs2)
    idx3 = unstriped8(offs3)
    idx4 = unstriped(offs4)
    idx5 = unstriped(offs5)
    idx6 = unstriped(offs6)
    idx7 = unstriped(offs7)
    xtu = unpack_weight(xt_words, xt_scales, "e4m3")
    wtu = unpack_weight(wt_words, wt_scales, "e2m1")
    wbu = unpack_weight(wb_words, wb_scales, "e5m2")
    wsu = unpack_weight(ws_words, ws_scales, "e5m2")
    wtidxg = wtu[:, idx]
    xtidx2g = xtu[:, idx2]
    a = wtidxg.T @ xtidx2g
    pw = np.zeros((R, C))
    pw[np.arange(R)[:, None], idx3[np.arange(R) % 512 // 64]] = a
    pg = np.maximum(pw, pw[:, idx4] * f64(sa))
    hid = pg[:, idx5]
    hidq = mxq(hid, 0, "e4m3")
    xtidx6g = xtu[:, idx6]
    p = wbu.T @ hidq + wsu.T @ xtidx6g
    y = np.zeros((N, E))
    y[:, idx7] = p
    return y

from contextlib import ExitStack

import concourse.mybir as mybir

K, T, J, R, V, C, O, N, E = 512, 1024, 256, 512, 1024, 512, 256, 256, 1024
FLOPS = 2 * K * R * J + 2 * R * N * O + 2 * K * N * O

F32 = mybir.dt.float32
BF16 = mybir.dt.bfloat16
I32 = mybir.dt.int32
U32 = mybir.dt.uint32
U16 = mybir.dt.uint16
U8 = mybir.dt.uint8
E4M3 = mybir.dt.float8_e4m3fn_x4
E5M2 = mybir.dt.float8_e5m2_x4
E2M1 = mybir.dt.float4_e2m1fn_x4
COPY = mybir.ActivationFunctionType.Copy

P = 128
PACK = 4
HALF = 128


def tile_list_ownladder_chosen_further_scattered_kernel(
    tc, xt_words, xt_scales, wt_words, wt_scales, sa, wb_words, wb_scales, ws_words, ws_scales,
    offs, offs2, offs3, offs4, offs5, offs6, offs7, out,
):
    nc = tc.nc
    with ExitStack() as ctx:
        lists = ctx.enter_context(tc.tile_pool(name="lists", bufs=1))
        keep = ctx.enter_context(tc.tile_pool(name="keep", bufs=1))
        turn = ctx.enter_context(tc.tile_pool(name="turn", bufs=1))
        psum = ctx.enter_context(tc.psum_pool(name="psum", bufs=1))

        def list_tile(name, src):
            return lists.tile([P, src.shape[1]], U16, name=name)

        def load_rows(queue, tl, src, quad):
            queue.dma_start(tl[32 * quad : 32 * quad + 4, :].bitcast(I32), src[0, 4 * quad : 4 * quad + 4, :].bitcast(I32))

        def load_words(queue, tl, src):
            queue.dma_start(tl[:].bitcast(I32), src[0].rearrange("p n t -> p (n t)").bitcast(I32))

        l_wt = list_tile("l_wt", offs)
        l_x2 = list_tile("l_x2", offs2)
        l_put = list_tile("l_put", offs3)
        l_look = list_tile("l_look", offs4)
        l_pick = list_tile("l_pick", offs5)
        l_x6 = list_tile("l_x6", offs6)
        l_out = list_tile("l_out", offs7)

        xt_pl = keep.tile([P, T], U8, name="xt_pl", align_bytes=64)
        wt_pl = turn.tile([P, V], U8, name="wt_pl", align_bytes=64, offset=1024)
        ws_pl = keep.tile([P, N], U8, name="ws_pl", align_bytes=64)
        wb_pl = keep.tile([P, N], U8, name="wb_pl", align_bytes=64)
        for tl in (xt_pl, wt_pl, ws_pl, wb_pl):
            nc.vector.memset(tl[:].bitcast(I32), 0)
        wt_w = keep.tile([P, V], U16, name="wt_w", align_bytes=64)
        xt_w = keep.tile([P, T], U32, name="xt_w", tag="page0", align_bytes=64)
        ws_w = keep.tile([P, N], U32, name="ws_w", align_bytes=64)
        wb_w = keep.tile([P, N], U32, name="wb_w", align_bytes=64)
        sa_t = keep.tile([P, PACK], F32, name="sa_t")
        boards = [keep.tile([P, C], F32, name="board%d" % t) for t in range(PACK)]
        for t in range(PACK):
            nc.vector.memset(boards[t][:], 0.0)

        nc.sync.dma_start(l_wt[:], offs)
        nc.scalar.dma_start(wt_w[:].bitcast(I32), wt_words[0].bitcast(I32))
        load_rows(nc.sync, xt_pl, xt_scales, 0)
        load_rows(nc.scalar, xt_pl, xt_scales, 1)
        load_rows(nc.sync, xt_pl, xt_scales, 2)
        load_rows(nc.scalar, xt_pl, xt_scales, 3)
        nc.sync.dma_start(l_x2[:], offs2)
        load_words(nc.scalar, xt_w, xt_words)
        nc.sync.dma_start(l_put[:], offs3)
        nc.sync.dma_start(l_look[:], offs4)
        load_rows(nc.scalar, wt_pl, wt_scales, 0)
        load_rows(nc.sync, wt_pl, wt_scales, 1)
        load_rows(nc.scalar, wt_pl, wt_scales, 2)
        load_rows(nc.sync, wt_pl, wt_scales, 3)
        nc.scalar.dma_start(sa_t[:], sa.rearrange("(p t) o -> p (t o)", t=PACK))
        nc.sync.dma_start(l_pick[:], offs5)
        nc.sync.dma_start(l_x6[:], offs6)
        load_words(nc.sync, ws_w, ws_words)
        for quad in range(4):
            load_rows(nc.sync, ws_pl, ws_scales, quad)
        load_words(nc.sync, wb_w, wb_words)
        for quad in range(4):
            load_rows(nc.sync, wb_pl, wb_scales, quad)
        nc.sync.dma_start(l_out[:], offs7)

        def halves(lst, h):
            return lst[:, 8 * h : 8 * h + 8]

        wt_g = keep.tile([P, R], U16, name="wt_g", align_bytes=64)
        nc.vector.tensor_copy(wt_g[:], wt_w[:].indirect(l_wt[:]))
        dealt = wt_g[:].rearrange("p (q t) -> p t q", t=PACK)
        wt_first = keep.tile([P, P], U16, name="wt_first", align_bytes=64)
        nc.vector.tensor_copy(wt_first[:], dealt[:, 0, :])
        x2_w0 = keep.tile([P, HALF], U32, name="x2_w0", align_bytes=64)
        x2_s0 = keep.tile([P, HALF], U8, name="x2_s0", align_bytes=64)
        nc.vector.tensor_copy(x2_w0[:], xt_w[:].indirect(halves(l_x2, 0)))
        nc.vector.tensor_copy(x2_s0[:], xt_pl[:].indirect(halves(l_x2, 0)))
        wt_gs = keep.tile([P, PACK, P], U8, name="wt_gs", align_bytes=64)
        nc.vector.tensor_copy(wt_gs[:].rearrange("p t q -> p q t"), wt_pl[:].indirect(l_wt[:]))
        wt_second = turn.tile([P, P], U16, name="wt_second", align_bytes=64, offset=1024)
        x2_w1 = turn.tile([P, HALF], U32, name="x2_w1", align_bytes=64, offset=1280)
        x2_s1 = turn.tile([P, HALF], U8, name="x2_s1", align_bytes=64, offset=1792)
        wt_rest = turn.tile([P, 2, P], U16, name="wt_rest", align_bytes=64, offset=1920)
        nc.vector.tensor_copy(wt_second[:], dealt[:, 1, :])
        nc.vector.tensor_copy(x2_w1[:], xt_w[:].indirect(halves(l_x2, 1)))
        nc.vector.tensor_copy(x2_s1[:], xt_pl[:].indirect(halves(l_x2, 1)))
        nc.vector.tensor_copy(wt_rest[:], dealt[:, 2:PACK, :])
        x2_w, x2_s = (x2_w0, x2_w1), (x2_s0, x2_s1)
        wt_rows = (wt_first[:], wt_second[:], wt_rest[:, 0, :], wt_rest[:, 1, :])

        hid = [keep.tile([P, HALF, PACK], BF16, name="hid%d" % h, align_bytes=64) for h in range(2)]
        prods = {}

        def product(acc, t, h):
            nc.tensor.matmul_mx(out=acc, lhsT=wt_rows[t].bitcast(E2M1), lhsT_scale=wt_gs[:, t, :],
                                rhs=x2_w[h][:].bitcast(E4M3), rhs_scale=x2_s[h][:], start=True, stop=True)

        def put_half(t, h, a_sb):
            nc.scalar.activation(boards[t][:].indirect(halves(l_put, h)), a_sb, COPY)

        def hidden(t, bank):
            acc = psum.tile([P, J], F32, name="acc", tag=bank)
            for h in range(2):
                product(acc[:, h * HALF : (h + 1) * HALF], t, h)
            a_sb = keep.tile([P, J], F32, name="a_sb", tag="a_sb%d" % t)
            nc.vector.tensor_copy(a_sb[:], acc[:])
            return a_sb

        def put(t, a_sb):
            nc.scalar.activation(boards[t][:].indirect(l_put[:]), a_sb[:], COPY)

        def look(t):
            for h in range(2):
                prod = keep.tile([P, C // 2], F32, name="prod%d_%d" % (t, h))
                nc.scalar.activation(prod[:], boards[t][:].indirect(l_look[:, 16 * h : 16 * h + 16]), COPY,
                                     scale=sa_t[:, t : t + 1])
                prods[t, h] = prod

        kept = [keep.tile([P, C], F32, name="kept%d" % t) for t in range(PACK)]

        def larger(t, h):
            cols = slice(h * C // 2, (h + 1) * C // 2)
            nc.vector.tensor_max(kept[t][:, cols], boards[t][:, cols], prods[t, h][:])

        def pick(t, h):
            nc.vector.tensor_copy(hid[h][:, :, t], kept[t][:].indirect(halves(l_pick, h)))

        sums = {}

        def short_way():
            x6_w = turn.tile([P, O], U32, name="x6_w", align_bytes=64, offset=768)
            x6_s = turn.tile([P, O], U8, name="x6_s", align_bytes=64, offset=1792)
            nc.vector.tensor_copy(x6_w[:], xt_w[:].indirect(l_x6[:]))
            nc.vector.tensor_copy(x6_s[:], xt_pl[:].indirect(l_x6[:]))
            for h in range(2):
                for n in range(2):
                    sums[n, h] = psum.tile([P, HALF], F32, name="sum%d_%d" % (n, h))
                    nc.tensor.matmul_mx(out=sums[n, h][:], lhsT=ws_w[:, n * P : (n + 1) * P].bitcast(E5M2),
                                        lhsT_scale=ws_pl[:, n * P : (n + 1) * P],
                                        rhs=x6_w[:, h * HALF : (h + 1) * HALF].bitcast(E4M3),
                                        rhs_scale=x6_s[:, h * HALF : (h + 1) * HALF], start=True, stop=False)

        def finish(h):
            codes = keep.tile([P, HALF], U32, name="codes%d" % h, align_bytes=64)
            cplane = keep.tile([P, HALF], U8, name="cplane%d" % h, align_bytes=64)
            nc.vector.quantize_mx(out=codes[:].bitcast(E4M3), scales=cplane[:],
                                  in_=hid[h][:].rearrange("p o t -> p (o t)"))
            for n in range(2):
                nc.tensor.matmul_mx(out=sums[n, h][:], lhsT=wb_w[:, n * P : (n + 1) * P].bitcast(E5M2),
                                    lhsT_scale=wb_pl[:, n * P : (n + 1) * P],
                                    rhs=codes[:].bitcast(E4M3), rhs_scale=cplane[:], start=False, stop=True)

        for t in range(2):
            acc = psum.tile([P, HALF], F32, name="acc_early", tag="bank%d" % t)
            product(acc[:], t, 0)
            a_early = keep.tile([P, HALF], F32, name="a_early%d" % t)
            if t == 0:
                nc.scalar.copy(a_early[:], acc[:])
            else:
                nc.vector.tensor_copy(a_early[:], acc[:])
            put_half(t, 0, a_early[:])
        acc = psum.tile([P, 2, HALF], F32, name="acc_late", tag="bank2")
        a_late = keep.tile([P, 2, HALF], F32, name="a_late")
        for t in range(2):
            product(acc[:, t, :], t, 1)
        nc.vector.tensor_copy(a_late[:], acc[:])
        for t in range(2):
            put_half(t, 1, a_late[:, t, :])
        put(2, hidden(2, "bank3"))
        last = hidden(3, "bank0")
        short_way()
        pages = [keep.tile([P, E], F32, name="page0", tag="page0", align_bytes=64),
                 turn.tile([P, E], F32, name="page1", align_bytes=64, offset=2368)]
        for n in range(2):
            nc.vector.memset(pages[n][:], 0.0)
        for t in range(2):
            look(t)
            larger(t, 0)
            larger(t, 1)
            pick(t, 0)
            pick(t, 1)
        put(3, last)
        look(2)
        look(3)
        larger(2, 0)
        larger(2, 1)
        pick(2, 0)
        larger(3, 0)
        larger(3, 1)
        pick(2, 1)
        pick(3, 0)
        pick(3, 1)
        finish(0)
        finish(1)

        for h in range(2):
            p0 = keep.tile([P, HALF], F32, name="p0_%d" % h)
            nc.scalar.copy(p0[:], sums[0, h][:])
            nc.scalar.activation(pages[0][:].indirect(halves(l_out, h)), p0[:], COPY)
            p1 = keep.tile([P, HALF], F32, name="p1_%d" % h)
            nc.vector.tensor_copy(p1[:], sums[1, h][:])
            nc.vector.tensor_copy(pages[1][:].indirect(halves(l_out, h)), p1[:])
        nc.scalar.dma_start(out[0:P, :], pages[0][:])
        nc.sync.dma_start(out[P : 2 * P, :], pages[1][:])
